import numpy as np, ml_dtypes
CORES = [3,7,11,15,131,135,139,143]
N = 8
RM, R, T = 262144, 8192, 2048
CAPP = 512
def entries(a): return a.T.reshape(-1)
def pack(v, P): return np.ascontiguousarray(np.asarray(v, np.int32).reshape(-1, P).T)
def owners(rng, how):
    if how == "alike": return np.stack([rng.permutation(np.repeat(rng.permutation(N)[:T // CAPP], CAPP)) for r in range(N)])
    if how == "full": p = np.repeat(rng.permutation(N)[:T // CAPP], CAPP); return np.stack([rng.permutation(p) for r in range(N)])
    return np.stack([rng.permutation(np.repeat(np.arange(N), CAPP))[:T] for r in range(N)])
def lists(rng, how):
    M = rng.integers(0, N * R, N * RM)
    O1 = owners(rng, how); O2 = rng.permutation(N)[O1] if how in ("alike", "full") else owners(rng, "uniform")
    sl = np.stack([1 + rng.permutation(RM - 2)[:N * T] for o in range(N)])
    if how == "edge": sl[:, 0] = 0; sl[:, 1] = RM - 1
    I = np.zeros((N, T), np.int64); took = np.zeros(N, np.int64)
    for r in range(N):
        for o in range(N): m = np.nonzero(O1[r] == o)[0]; I[r, m] = RM * o + sl[o, took[o]:took[o] + len(m)]; took[o] += len(m)
    A = R * O2 + (np.where(rng.random((N, T)) < 0.5, 0, R - 1) if how == "edge" else rng.integers(0, R, (N, T)))
    if how == "alike": I = RM * O1 + sl[O1, 0]; A = R * O2 + rng.integers(0, R, N)[O1]
    M[I.reshape(-1)] = A.reshape(-1)
    if how == "sorted": I = np.sort(I, axis=1)
    if how == "full":
        I[1::3] = np.sort(I[1::3], axis=1); I[2::3] = np.sort(I[2::3], axis=1).reshape(-1, 16, T // 16).transpose(0, 2, 1).reshape(-1, T)
    return {"mp": np.stack([pack(m, 16) for m in M.reshape(N, RM)]), "idx": np.stack([pack(i, 16) for i in I])}
def setup_inputs(rng):
    return dict({"tab": rng.standard_normal((N, 128, R), dtype=np.float32).astype(ml_dtypes.bfloat16)}, **lists(rng, "uniform"))
def setup_inputs_alike(rng):
    d = setup_inputs(rng); d.update(lists(rng, "alike"))
    for k in ("tab",): d[k] = (d[k].astype(np.float32) * 1048576.0).astype(d[k].dtype)
    return d
def setup_inputs_edge(rng):
    d = setup_inputs(rng); d.update(lists(rng, "edge"))
    for k in ("tab",): d[k] = (d[k].astype(np.float32) * (1 / 1024.0)).astype(d[k].dtype)
    return d
def setup_inputs_full(rng):
    d = setup_inputs(rng); d.update(lists(rng, "full"))
    return d
def setup_inputs_sorted(rng):
    d = setup_inputs(rng); d.update(lists(rng, "sorted"))
    return d
def check_inputs(x):
    bad = []
    if x["mp"].min() < 0 or x["mp"].max() >= N * R: bad.append("mp out of range")
    if x["idx"].min() < 0 or x["idx"].max() >= N * RM: bad.append("idx out of range")
    M = np.concatenate([entries(m) for m in x["mp"]])
    if max(int(np.bincount(entries(a) // RM, minlength=N).max()) for a in x["idx"]) > CAPP: bad.append("more than CAPP entries of a list point into one rank's part of the map")
    if max(int(np.bincount(M[entries(a)] // R, minlength=N).max()) for a in x["idx"]) > CAPP: bad.append("more than CAPP entries of a list have map values in one rank's part of the table")
    return bad
def reference(tab, mp, idx):
    A = np.concatenate(list(tab), axis=1)
    M = np.concatenate([entries(m) for m in mp])
    return {"y": np.stack([A[:, M[entries(idx[r])]] for r in range(N)])}

@@ -1,0 +1,422 @@
+from concourse.bass import DstId, RemoteDMATransfer
+from concourse.mybir import AluOpType as OP, ActivationFunctionType as AF
+
+F, B, I, U = "float32", "bfloat16", "int32", "uint16"
+SCRATCH = {
+    "ci": ("sbuf", [128, 64], I), "cf": ("sbuf", [128, 40], F), "cb": ("sbuf", [128, 1408], B), "c5": ("sbuf", [128, 1024], B),
+    "cg": ("sbuf", [128, 256], F), "cu": ("sbuf", [128, 40], U), "LU": ("sbuf", [128, 512], B), "wc": ("sbuf", [128, 16], B),
+    "mpw": ("sbuf", [128, 8200], I), "tabw": ("sbuf", [128, 8192], B),
+    "E": ("sbuf", [128, 16], I), "VAL": ("sbuf", [128, 16], I),
+    "O": ("sbuf", [128, 16], I), "mk": ("sbuf", [128, 128], B), "inc": ("sbuf", [128, 128], B), "sl": ("sbuf", [128, 128], F),
+    "ta": ("sbuf", [128, 64], F), "tb": ("sbuf", [128, 32], F), "S": ("sbuf", [128, 16], I), "KI": ("sbuf", [128, 32], I),
+    "KF": ("sbuf", [128, 32], F), "VI": ("sbuf", [128, 32], I), "VF": ("sbuf", [128, 32], F), "A": ("sbuf", [128, 2048], B),
+    "Bt": ("sbuf", [128, 1024], B), "Bo": ("sbuf", [128, 1024], B), "W": ("sbuf", [128, 64], B),
+    "XS": ("sbuf", [128, 64], I), "XL": ("sbuf", [128, 64], I), "oi": ("sbuf", [128, 128], I), "off": ("sbuf", [128, 64], U),
+    "rid": ("sbuf", [128, 64], U), "mm": ("sbuf", [128, 1024], B), "xm": ("sbuf", [128, 1024], F),
+    "VS": ("sbuf", [128, 32], F), "VL": ("sbuf", [128, 32], F),
+    "kk": ("sbuf", [128, 64], I), "kj": ("sbuf", [128, 32], F), "AJ": ("sbuf", [128, 2048], B), "AT": ("sbuf", [128, 2048], B),
+    "BN": ("sbuf", [128, 512], B), "vv": ("sbuf", [128, 64], B), "prod": ("sbuf", [128, 512], F), "acc": ("sbuf", [128, 512], F),
+    "LS": ("sbuf", [128, 256], U), "TL": ("sbuf", [128, 256], U), "rf": ("sbuf", [128, 128], F), "fin": ("sbuf", [128, 128], U),
+    "SB": ("sbuf", [128, 4096], B), "D2": ("sbuf", [128, 4096], B), "Y": ("sbuf", [128, 2048], B),
+    "PA": ("psum", [128, 512], F), "PB": ("psum", [128, 512], F), "PC": ("psum", [128, 512], F),
+    "PF": ("psum", [128, 1024], F), "PX": ("psum", [128, 512], F), "PT": ("psum", [128, 2048], B),
+}
+SEMAPHORES = ["ev", "ea", "ep", "eg", "li", "lm", "lt", "st", "ax", "av", "ad", "s1", "s2", "s3", "s4"] + ["al%d" % _i for _i in range(8)]
+
+
+def rank_program(g, core, T, topo):
+    me = T.rank_of(core)
+    if me is None:
+        return
+    cores, N = T.cores, len(T.cores)
+    eng = {"v": g.vector, "a": g.scalar, "p": g.tensor, "g": g, "s": g.sync}
+    cnt = {"v": 0, "a": 0, "p": 0, "g": 0}
+    seen = {}
+
+    def need(q, *toks):
+        for name, val in toks:
+            if seen.get((q, name), 0) < val:
+                eng[q].wait_ge(T.sem[name], val)
+                seen[(q, name)] = val
+
+    def done(q, ins):
+        cnt[q] += 1
+        ins.then_inc(T.sem["e" + q], 1)
+        return ("e" + q, cnt[q])
+
+    def now(q):
+        return ("e" + q, cnt[q])
+
+    def ts(out, in0, s1, s2, op0, op1=None):
+        if op1 is None:
+            return done("v", g.vector.tensor_scalar(out, in0, s1, s2, op0))
+        return done("v", g.vector.tensor_scalar(out, in0, s1, s2, op0, op1))
+
+    def tt(out, a, b, op):
+        return done("v", g.vector.tensor_tensor(out, a, b, op))
+
+    def cp(out, a):
+        return done("v", g.vector.tensor_copy(out, a))
+
+    def act(out, a, f, **kw):
+        return done("a", g.scalar.activation(out, a, f, **kw))
+
+    def mat(out, l, r, start=True, stop=True):
+        return g.tensor.matmul(out, l, r, start, stop)
+
+    def same_chip(a, b):
+        return topo.host(a) == topo.host(b) and topo.chip(a) == topo.chip(b)
+
+    def order(r):
+        c = cores[r]
+        both, sw, mate, chip = [], [], [], []
+        for k in range(1, N):
+            s = (r + k) % N
+            d = cores[s]
+            (chip if same_chip(c, d) else mate if topo.mates(c, d) else sw if topo.same_plane(c, d) else both).append(s)
+        return both + [x for p in zip(sw, mate) for x in p] + chip + [r]
+    ords = [order(r) for r in range(N)]
+    mine = ords[me]
+
+    def pos(o, r):
+        return ords[o].index(r)
+
+    def bits(m):
+        return [1 << i for i in range(16) if m >> i & 1]
+
+    far = [r for r in mine if r != me and not same_chip(core, cores[r])]
+    near = [r for r in mine if r != me and same_chip(core, cores[r])]
+    eoff = bits(topo.mask(core, cores[far[0]]))
+    eon = [e for e in bits(topo.mask(core, cores[near[0]])) if e not in eoff][:4]
+    groups = [(far[:4], 2), (far[4:], 4)]
+
+    def engines_for(src, dst):
+        o = [r for r in ords[src] if r != src and not same_chip(cores[src], cores[r])]
+        return 2 if dst in o[:4] else 4
+
+    def fused(jobs, sem, local):
+        tr, tot = [], 0
+        for r, es, s, d in jobs:
+            rid, pnc = topo.addr(cores[r], core)
+            tr.append(RemoteDMATransfer(dst_ids=[DstId(rid=rid, pnc=pnc)], dma_engine_mask=sum(es), remote_sem=T.sem[sem(r)], src=s, dst=d))
+            tot += len(es)
+        g.remote_dma_fused(tr, local_sem=T.sem[local])
+        return tot
+
+    def control(which, item, sem, local):
+        ds, w = groups[which]
+        jobs = [(r, eoff[i * w:(i + 1) * w]) + item(r) for i, r in enumerate(ds)]
+        if which == 1:
+            jobs += [(r, eon) + item(r) for r in near]
+        return fused(jobs, sem, local)
+    arrive = sum(engines_for(s, me) for s in range(N) if s != me)
+
+    g.sync.dma_start(T.E[:], T.idx[:]).then_inc(T.sem.li, 16)
+    for v in range(2):
+        for u in range(4):
+            p0 = 32 * u + 16 * v
+            g.sync.dma_start(T.mpw[p0:p0 + 16, 4:8196], T.mp[:, 8192 * v:8192 * v + 8192]).then_inc(T.sem.lm, 16)
+
+    names = ["cO", "c4O", "cT", "rst", "i128", "neg1", "ntri", "ident", "ckA", "L2", "ones"]
+    C = {n: T.cb[:, 128 * i:128 * i + 128] for i, n in enumerate(names)}
+    ones = C["ones"]
+    i64 = T.cb[:, 128 * names.index("i128"):128 * names.index("i128") + 64]
+    i4 = T.cb[:, 128 * names.index("i128"):128 * names.index("i128") + 4]
+    pint, pint1, rep1i, repi = T.ci[:, 0:8], T.ci[:, 0:1], T.ci[:, 16:24], T.ci[:, 32:64]
+
+    def pbit(k):
+        return T.ci[:, 8 + k:9 + k]
+
+    def pcol(k):
+        return T.cf[:, k:k + 1]
+    w512, w256, cst, selu = T.cf[:, 8:9], T.cf[:, 9:10], T.cf[:, 10:11], T.cf[:, 12:16]
+    i32r, rst32 = T.c5[:, 0:512], T.c5[:, 512:1024]
+    mskb, self32 = T.cg[:, 0:128], T.cg[:, 128:256]
+    rep1, repn = T.cu[:, 0:8], T.cu[:, 8:40]
+
+    def iota(buf, pattern, base, cm):
+        return done("g", g.iota(buf, pattern, base, cm, allow_small_or_imprecise_dtypes=True))
+    m_neg = done("v", g.vector.memset(C["neg1"], -1.0))
+    m_ones = done("v", g.vector.memset(ones, 1.0))
+    done("v", g.vector.memset(T.mpw[:, 3:4], 0))
+    m_zero = done("v", g.vector.memset(T.mpw[:, 8196:8197], 0))
+    k_pint = iota(pint, [[0, 8]], 0, 1)
+    k_cO = iota(C["cO"], [[1, 8], [0, 16]], 0, 0)
+    k_cT = iota(C["cT"], [[0, 8], [1, 16]], 0, 0)
+    need("g", m_neg)
+    k_ntri = done("g", g.affine_select(C["ntri"], C["neg1"], [[-1, 128]], OP.is_ge, 0.0, 0, 1))
+    k_i128 = iota(C["i128"], [[1, 128]], 0, 0)
+    k_ckA = iota(C["ckA"], [[16, 4], [0, 2], [1, 16]], 0, 0)
+    need("g", m_ones)
+    k_id = done("g", g.affine_select(C["ident"], ones, [[-1, 128]], OP.is_equal, 0.0, 0, 1))
+    k_repi = iota(repi, [[1, 16], [0, 2]], 0, 0)
+
+    need("v", k_pint)
+    t_r1 = ts(rep1i, pint, 15, None, OP.bitwise_and)
+    ts(pbit(0), pint1, 63, None, OP.bitwise_and)
+    ts(pbit(1), pint1, 4, 1, OP.logical_shift_right, OP.bitwise_and)
+    ts(pbit(2), pint1, 5, None, OP.logical_shift_right)
+    ts(pbit(3), pint1, 7, None, OP.bitwise_and)
+    ts(pbit(4), pint1, 3, None, OP.logical_shift_right)
+    ts(pbit(5), pint1, 6, None, OP.logical_shift_right)
+    t_pb = ts(T.ci[:, 14:16], T.ci[:, 0:2], 15, None, OP.bitwise_and)
+    need("v", t_pb)
+    t_rep1 = cp(rep1, rep1i)
+    t_pc = cp(T.cf[:, 0:8], T.ci[:, 8:16])
+    need("v", k_cO)
+    k_c4O = ts(C["c4O"], C["cO"], 4.0, None, OP.mult)
+    need("v", t_pc)
+    ts(w256, pcol(5), -255.0, 256.0, OP.mult, OP.add)
+    t_w = ts(w512, pcol(5), -511.0, 512.0, OP.mult, OP.add)
+    t_cst = ts(cst, pcol(1), -131072.0, 131344.0, OP.mult, OP.add)
+    need("v", k_cT)
+    t_rst = ts(C["rst"], C["cT"], 1.0, None, OP.min)
+
+    def compact(P, tok, oshift, values, onesb):
+        KF, VF, A, Bt, Bo = T.KF, T.VF, T.A, T.Bt, T.Bo
+        need("v", tok)
+        x = ts(T.O[:], P[:], oshift, None, OP.logical_shift_right)
+        need("v", x, t_rep1, k_cO)
+        k = tt(T.mk[:], T.O[:, 0:16].indirect(rep1), C["cO"], OP.is_equal)
+        need("v", k, t_rst)
+        n = done("v", g.vector.tensor_tensor_scan(T.inc[:], C["rst"], T.mk[:], 0.0, OP.mult, OP.add))
+        need("p", m_ones, k_c4O, k_ntri, k)
+        mat(T.PA[:, 0:128], onesb, C["c4O"], True, False)
+        mat(T.PA[:, 0:128], C["ntri"], T.mk[:], False, False)
+        need("p", n)
+        r = done("p", mat(T.PA[:, 0:128], onesb, T.inc[:], False, True))
+        values(T.VI, VF)
+        need("v", r)
+        x = tt(T.sl[:], T.mk[:], T.PA[:, 0:128], OP.mult)
+        need("v", x)
+        x = tt(T.ta[:], T.sl[:, 0:64], T.sl[:, 64:128], OP.add)
+        need("v", x)
+        x = tt(T.tb[:], T.ta[:, 0:32], T.ta[:, 32:64], OP.add)
+        need("v", x)
+        x = tt(T.S[:], T.tb[:, 0:16], T.tb[:, 16:32], OP.add)
+        need("v", x)
+        ts(T.KI[:, 16:32], T.S[:], 6, None, OP.logical_shift_right)
+        x = ts(T.KI[:, 0:16], T.S[:], 63, None, OP.bitwise_and)
+        need("v", x)
+        kf = cp(KF[:], T.KI[:])
+        need("a", kf, k_i128)
+        chunks = [(2, 6), (6, 10), (10, 14), (14, 16)]
+        btok = {}
+
+        def absolutes(c):
+            for t in range(*chunks[c]):
+                x = act(Bt[:, 64 * t:64 * t + 64], i64, AF.Abs, bias=KF[:, 16 + t:17 + t], scale=-1.0)
+            return x
+        xs = [absolutes(0)]
+        for c in range(4):
+            if c < 3:
+                xs.append(absolutes(c + 1))
+            need("a", xs[c])
+            a, b = chunks[c]
+            x = act(Bo[:, 64 * a:64 * b], Bt[:, 64 * a:64 * b], AF.Relu, bias=1.0, scale=-1.0)
+            for t in range(a, b):
+                btok[t] = x
+        need("v", kf, k_i128)
+        atok = {}
+        for t in range(16):
+            ts(A[:, 128 * t:128 * t + 64], i64, KF[:, t:t + 1], VF[:, 16 + t:17 + t], OP.is_equal, OP.mult)
+            if t not in btok:
+                ts(Bo[:, 64 * t:64 * t + 64], i64, KF[:, 16 + t:17 + t], None, OP.is_equal)
+            atok[t] = ts(A[:, 128 * t + 64:128 * t + 128], i64, KF[:, t:t + 1], VF[:, t:t + 1], OP.is_equal, OP.mult)
+        for t in range(16):
+            need("p", atok[t])
+            if t in btok:
+                need("p", btok[t])
+            m = mat(T.PB[:, 0:64], A[:, 128 * t:128 * t + 128], Bo[:, 64 * t:64 * t + 64], t == 0, t == 15)
+        m = done("p", m)
+        need("v", m)
+        return cp(T.W[:], T.PB[:, 0:64])
+
+    def values1(VI, VF):
+        ts(VI[:, 0:16], T.E[:], 511, None, OP.bitwise_and)
+        x = ts(VI[:, 16:32], T.E[:], 9, 511, OP.logical_shift_right, OP.bitwise_and)
+        need("v", x)
+        ts(VF[:], VI[:], -256.0, None, OP.add)
+        need("v", t_w, k_ckA)
+        x = ts(C["L2"], C["ckA"], pcol(0), w512, OP.is_equal, OP.mult)
+        need("v", x)
+
+    w1 = compact(T.E, ("li", 16), 18, values1, ones)
+    need("p", w1)
+    x = done("p", mat(T.PC[:, 0:64], C["L2"], T.W[:]))
+    need("v", x, t_cst)
+    x1 = ts(T.XS[:], T.PC[:, 0:64], cst, None, OP.add)
+    need("g", x1)
+    tot = 0
+    for w in range(2):
+        tot += control(w, lambda r: (T.XS[:, 8 * r:8 * r + 8], T.XL[:, 8 * pos(r, me):8 * pos(r, me) + 8]), lambda r: "ax", "s1")
+    k_i32 = iota(i32r, [[0, 16], [1, 32]], 0, 0)
+    need("v", x1)
+    own = cp(T.XL[:, 56:64], T.XS[:, 8 * me:8 * me + 8])
+    need("s", ("s1", tot))
+    g.sync.dma_start(T.tabw[:, 0:4096], T.tab[:, 0:4096]).then_inc(T.sem.lt, 16)
+
+    ts(T.kk[:, 0:16], T.S[:], 2, 112, OP.logical_shift_right, OP.bitwise_and)
+    ts(T.kk[:, 16:32], T.S[:], 7, 28, OP.logical_shift_right, OP.bitwise_and)
+    ts(T.kk[:, 32:48], T.S[:], 15, None, OP.bitwise_and)
+    x = ts(T.kk[:, 48:64], T.S[:], 4, 3, OP.logical_shift_right, OP.bitwise_and)
+    need("v", x)
+    x = tt(T.kj[:], T.kk[:, 0:32], T.kk[:, 32:64], OP.add)
+    ts(selu, i4, pcol(2), None, OP.is_equal)
+    k_wc = ts(T.wc[:], C["cT"][:, 0:16], pcol(6), None, OP.is_equal)
+    need("v", k_repi)
+    rn = cp(repn, repi)
+    need("v", x)
+    jt = []
+    for t in range(16):
+        jt.append(ts(T.AJ[:, 128 * t:128 * t + 128], C["i128"], T.kj[:, t:t + 1], None, OP.is_equal))
+    at = []
+    need("p", k_id)
+    for rd in range(2):
+        for t in range(8 * rd, 8 * rd + 8):
+            need("p", jt[t])
+            m = g.tensor.transpose(T.PT[:, 128 * t:128 * t + 128], T.AJ[:, 128 * t:128 * t + 128], C["ident"])
+        m = done("p", m)
+        a, b = 1024 * rd, 1024 * rd + 1024
+        if rd:
+            need("v", m)
+            at.append(cp(T.AT[:, a:b], T.PT[:, a:b]))
+        else:
+            need("a", m)
+            at.append(act(T.AT[:, a:b], T.PT[:, a:b], AF.Copy))
+
+    need("v", ("ax", arrive), own)
+    ri = ts(T.oi[:, 0:64], T.XL[:], 15, None, OP.bitwise_and)
+    ci = ts(T.oi[:, 64:128], T.XL[:], 4, None, OP.arith_shift_right)
+    need("v", ri)
+    rd = cp(T.rid[:], T.oi[:, 0:64])
+    need("v", ci)
+    of = ts(T.off[:], T.oi[:, 64:128], 0.0, 8193.0, OP.max, OP.min)
+    need("a", rd, k_wc)
+    parts = [(0, 1), (1, 2), (2, 4), (4, 6), (6, 8)]
+    mt = [act(T.mm[:, 128 * a:128 * b], T.wc[:, 0:16].indirect(T.rid[:, 8 * a:8 * b]), AF.Copy) for a, b in parts]
+    need("v", of, ("lm", 128), m_zero)
+    ft = []
+    for (a, b), m in zip(parts, mt):
+        need("v", m)
+        x = tt(T.xm[:, 128 * a:128 * b], T.mpw[:, 3:8197].indirect(T.off[:, 8 * a:8 * b]), T.mm[:, 128 * a:128 * b], OP.mult)
+        need("p", x)
+        for r in range(a, b):
+            PV = T.PA if r >= 4 else T.PB
+            m = mat(PV[:, 4 * (r % 4):4 * (r % 4) + 4], T.xm[:, 128 * r:128 * r + 128], selu)
+        if b in (4, 8):
+            ft.append(done("p", m))
+    s2tot = 0
+    for h in range(2):
+        PV = T.PA if h else T.PB
+        need("a", ft[h])
+        vs = act(T.VS[:, 16 * h:16 * h + 16], PV[:, 0:16], AF.Copy)
+        need("g", vs)
+        s2tot += control(h, lambda r: (T.VS[:, 4 * mine.index(r):4 * mine.index(r) + 4], T.VL[:, 4 * me:4 * me + 4]), lambda r: "av", "s2")
+    need("s", ("s2", s2tot))
+    g.sync.dma_start(T.tabw[:, 4096:8192], T.tab[:, 4096:8192]).then_inc(T.sem.lt, 16)
+    need("v", vs)
+    own = cp(T.VL[:, 4 * me:4 * me + 4], T.VS[:, 28:32])
+
+    need("v", rn, k_i32)
+    bn = tt(T.BN[:], T.kj[:, 16:32].indirect(repn), i32r, OP.is_equal)
+    r32 = ts(rst32, i32r, 1.0, None, OP.min)
+    for u in range(4):
+        x = ts(T.cf[:, 32 + u:33 + u], pcol(0), float(-16 * u), None, OP.add)
+    need("v", x)
+    for u in range(4):
+        ts(T.LU[:, 128 * u:128 * u + 128], C["cT"], T.cf[:, 32 + u:33 + u], w256, OP.is_equal, OP.mult)
+    ts(mskb, C["cO"], pcol(3), None, OP.is_equal)
+    k_late = ts(self32, C["cT"], pcol(4), None, OP.is_equal)
+
+    vh, vl = T.vv[:, 0:32], T.vv[:, 32:64]
+    need("v", ("av", arrive), own)
+    x = cp(vh, T.VL[:])
+    need("v", x)
+    x = tt(vl, T.VL[:], vh, OP.subtract)
+    need("p", x, *at)
+    PQ = [T.PF[:, 0:128], T.PX[:, 0:128], T.PF[:, 512:640], T.PC[:, 0:128]]
+    zt = []
+    for t in range(16):
+        z = PQ[t // 4][:, 32 * (t % 4):32 * (t % 4) + 32]
+        mat(z, T.AT[:, 128 * t:128 * t + 128], vh, True, False)
+        m = mat(z, T.AT[:, 128 * t:128 * t + 128], vl, False, True)
+        if t % 4 == 3:
+            zt.append(done("p", m))
+    need("v", bn, r32)
+    for k in range(4):
+        c0, c1 = 128 * k, 128 * k + 128
+        need("v", zt[k])
+        x = tt(T.prod[:, c0:c1], T.BN[:, c0:c1], PQ[k], OP.mult)
+        need("v", x)
+        x = done("v", g.vector.tensor_tensor_scan(T.acc[:, c0:c1], rst32[:, c0:c1], T.prod[:, c0:c1], 0.0, OP.mult, OP.add))
+    need("v", x)
+    val = cp(T.VAL[:], T.acc[:, 31:512:32])
+
+    def values2(VI, VF):
+        ts(VI[:, 0:16], T.VAL[:], 255, None, OP.bitwise_and)
+        x = ts(VI[:, 16:32], T.VAL[:], 8, 31, OP.logical_shift_right, OP.bitwise_and)
+        need("v", x)
+        x = cp(VF[:], VI[:])
+        need("v", x)
+
+    need("p", k_late)
+    w2 = compact(T.VAL, val, 13, values2, ones)
+    need("p", w2)
+    for u in range(4):
+        m = mat(T.PC[:, u:256:4], T.LU[:, 128 * u:128 * u + 128], T.W[:])
+    m = done("p", m)
+    need("v", m)
+    ls = cp(T.LS[:], T.PC[:, 0:256])
+    need("g", ls)
+    s3tot = 0
+    for w in range(2):
+        s3tot += control(w, lambda r: (T.LS[:, 32 * r:32 * r + 32], T.TL[:, 32 * pos(r, me):32 * pos(r, me) + 32]), lambda r: "al%d" % pos(r, me), "s3")
+    x = tt(T.rf[:], T.S[:, 0:16].indirect(rep1), mskb, OP.mult)
+    need("p", x)
+    m = done("p", mat(T.PA[:, 0:128], self32, T.rf[:]))
+    need("v", m)
+    fin = cp(T.fin[:], T.PA[:, 0:128])
+
+    sent = 0
+    for i in range(2):
+        r, toks = mine[i], []
+        for k in range(2):
+            q = "va"[k]
+            need(q, ("al%d" % i, engines_for(r, me)), ("lt", 32))
+            c0 = 512 * i + 256 * k
+            win, out = T.tabw[:, 0:8192].indirect(T.TL[:, c0 // 16:c0 // 16 + 16]), T.SB[:, c0:c0 + 256]
+            toks.append(cp(out, win) if q == "v" else act(out, win, AF.Copy))
+        need("g", *toks)
+        sent += fused([(r, eoff[i::2], T.SB[:, 512 * i:512 * i + 512], T.D2[:, 512 * me:512 * me + 512])], lambda r: "ad", "s4")
+    for i in range(2, 8, 2):
+        jobs, toks = [], []
+        for k in range(2):
+            r, q = mine[i + k], "va"[k]
+            if r == me:
+                need(q, ls)
+                lst, out = T.LS[:, 32 * me:32 * me + 32], T.D2[:, 512 * me:512 * me + 512]
+            else:
+                need(q, ("al%d" % (i + k), engines_for(r, me)))
+                lst, out = T.TL[:, 32 * (i + k):32 * (i + k) + 32], T.SB[:, 512 * (i + k):512 * (i + k) + 512]
+                jobs.append((r, eon if r in near else eoff[k::2], out, T.D2[:, 512 * me:512 * me + 512]))
+            win = T.tabw[:, 0:8192].indirect(lst)
+            x = cp(out, win) if q == "v" else act(out, win, AF.Copy)
+            if r == me:
+                dself = x
+            else:
+                toks.append(x)
+        need("g", *toks)
+        sent += fused(jobs, lambda r: "ad", "s4")
+    dat = sum(len(eoff) // 2 if not same_chip(cores[s], core) else len(eon) for s in range(N) if s != me)
+
+    for i, (c0, c1) in enumerate([(0, 640), (640, 1280), (1280, 1664), (1664, 2048)]):
+        q = "va"[i % 2]
+        need(q, dself, fin, ("ad", dat))
+        win = T.D2[:, 0:4096].indirect(T.fin[:, c0 // 16:c1 // 16])
+        out = T.Y[:, c0:c1]
+        x = cp(out, win) if q == "v" else act(out, win, AF.Copy)
+        need("s", x)
+        g.sync.dma_start(T.y[:, c0:c1], out).then_inc(T.sem.st, 16)
+    need("s", ("st", 64))
+    need("g", ("s2", s2tot), ("s3", s3tot), ("s4", sent), now("v"), now("a"), now("p"), now("g"))

@@ -10,7 +10,7 @@ SCRATCH = {
     "O": ("sbuf", [128, 16], I), "mk": ("sbuf", [128, 128], B), "inc": ("sbuf", [128, 128], B), "sl": ("sbuf", [128, 128], F),
     "ta": ("sbuf", [128, 64], F), "tb": ("sbuf", [128, 32], F), "S": ("sbuf", [128, 16], I), "KI": ("sbuf", [128, 32], I),
     "KF": ("sbuf", [128, 32], F), "VI": ("sbuf", [128, 32], I), "VF": ("sbuf", [128, 32], F), "A": ("sbuf", [128, 2048], B),
-    "Bt": ("sbuf", [128, 1024], B), "Bo": ("sbuf", [128, 1024], B), "W": ("sbuf", [128, 64], B),
+    "ih": ("sbuf", [128, 72], B), "Bo": ("sbuf", [128, 1152], B), "WS": ("sbuf", [128, 64], F), "W": ("sbuf", [128, 64], B),
     "XS": ("sbuf", [128, 64], I), "XL": ("sbuf", [128, 64], I), "oi": ("sbuf", [128, 128], I), "off": ("sbuf", [128, 64], U),
     "rid": ("sbuf", [128, 64], U), "mm": ("sbuf", [128, 1024], B), "xm": ("sbuf", [128, 1024], F),
     "VS": ("sbuf", [128, 32], F), "VL": ("sbuf", [128, 32], F),
@@ -146,6 +146,7 @@ def rank_program(g, core, T, topo):
     need("g", m_neg)
     k_ntri = done("g", g.affine_select(C["ntri"], C["neg1"], [[-1, 128]], OP.is_ge, 0.0, 0, 1))
     k_i128 = iota(C["i128"], [[1, 128]], 0, 0)
+    k_ih = iota(T.ih[:], [[2, 72]], -1, 0)
     k_ckA = iota(C["ckA"], [[16, 4], [0, 2], [1, 16]], 0, 0)
     need("g", m_ones)
     k_id = done("g", g.affine_select(C["ident"], ones, [[-1, 128]], OP.is_equal, 0.0, 0, 1))
@@ -166,14 +167,14 @@ def rank_program(g, core, T, topo):
     need("v", k_cO)
     k_c4O = ts(C["c4O"], C["cO"], 4.0, None, OP.mult)
     need("v", t_pc)
-    ts(w256, pcol(5), -255.0, 256.0, OP.mult, OP.add)
-    t_w = ts(w512, pcol(5), -511.0, 512.0, OP.mult, OP.add)
+    ts(w256, pcol(5), -127.5, 128.0, OP.mult, OP.add)
+    t_w = ts(w512, pcol(5), -255.5, 256.0, OP.mult, OP.add)
     t_cst = ts(cst, pcol(1), -131072.0, 131344.0, OP.mult, OP.add)
     need("v", k_cT)
     t_rst = ts(C["rst"], C["cT"], 1.0, None, OP.min)
 
     def compact(P, tok, oshift, values, onesb):
-        KF, VF, A, Bt, Bo = T.KF, T.VF, T.A, T.Bt, T.Bo
+        KF, VF, A, Bo = T.KF, T.VF, T.A, T.Bo
         need("v", tok)
         x = ts(T.O[:], P[:], oshift, None, OP.logical_shift_right)
         need("v", x, t_rep1, k_cO)
@@ -199,38 +200,21 @@ def rank_program(g, core, T, topo):
         x = ts(T.KI[:, 0:16], T.S[:], 63, None, OP.bitwise_and)
         need("v", x)
         kf = cp(KF[:], T.KI[:])
-        need("a", kf, k_i128)
-        chunks = [(2, 6), (6, 10), (10, 14), (14, 16)]
-        btok = {}
-
-        def absolutes(c):
-            for t in range(*chunks[c]):
-                x = act(Bt[:, 64 * t:64 * t + 64], i64, AF.Abs, bias=KF[:, 16 + t:17 + t], scale=-1.0)
-            return x
-        xs = [absolutes(0)]
-        for c in range(4):
-            if c < 3:
-                xs.append(absolutes(c + 1))
-            need("a", xs[c])
-            a, b = chunks[c]
-            x = act(Bo[:, 64 * a:64 * b], Bt[:, 64 * a:64 * b], AF.Relu, bias=1.0, scale=-1.0)
-            for t in range(a, b):
-                btok[t] = x
+        need("a", kf, k_ih)
+        btok = [act(Bo[:, 72 * t:72 * t + 65], T.ih[:, 0:65], AF.Sign, bias=KF[:, 16 + t:17 + t], scale=-0.5) for t in range(16)]
         need("v", kf, k_i128)
-        atok = {}
+        atok = []
         for t in range(16):
             ts(A[:, 128 * t:128 * t + 64], i64, KF[:, t:t + 1], VF[:, 16 + t:17 + t], OP.is_equal, OP.mult)
-            if t not in btok:
-                ts(Bo[:, 64 * t:64 * t + 64], i64, KF[:, 16 + t:17 + t], None, OP.is_equal)
-            atok[t] = ts(A[:, 128 * t + 64:128 * t + 128], i64, KF[:, t:t + 1], VF[:, t:t + 1], OP.is_equal, OP.mult)
+            atok.append(ts(A[:, 128 * t + 64:128 * t + 128], i64, KF[:, t:t + 1], VF[:, t:t + 1], OP.is_equal, OP.mult))
         for t in range(16):
-            need("p", atok[t])
-            if t in btok:
-                need("p", btok[t])
-            m = mat(T.PB[:, 0:64], A[:, 128 * t:128 * t + 128], Bo[:, 64 * t:64 * t + 64], t == 0, t == 15)
+            need("p", atok[t], btok[t])
+            m = mat(T.PB[:, 0:65], A[:, 128 * t:128 * t + 128], Bo[:, 72 * t:72 * t + 65], t == 0, t == 15)
         m = done("p", m)
         need("v", m)
-        return cp(T.W[:], T.PB[:, 0:64])
+        x = cp(T.WS[:], T.PB[:, 0:64])
+        need("v", x)
+        return tt(T.W[:], T.WS[:], T.PB[:, 1:65], OP.subtract)
 
     def values1(VI, VF):
         ts(VI[:, 0:16], T.E[:], 511, None, OP.bitwise_and)

from concourse.bass import DstId, RemoteDMATransfer
from concourse.mybir import AluOpType as OP, ActivationFunctionType as AF

F, B, I, U = "float32", "bfloat16", "int32", "uint16"
SCRATCH = {
    "ci": ("sbuf", [128, 64], I), "cf": ("sbuf", [128, 40], F), "cb": ("sbuf", [128, 1408], B), "c5": ("sbuf", [128, 1024], B),
    "cg": ("sbuf", [128, 256], F), "cu": ("sbuf", [128, 40], U), "LU": ("sbuf", [128, 512], B), "wc": ("sbuf", [128, 16], B),
    "mpw": ("sbuf", [128, 8200], I), "tabw": ("sbuf", [128, 8192], B),
    "E": ("sbuf", [128, 16], I), "VAL": ("sbuf", [128, 16], I),
    "O": ("sbuf", [128, 16], I), "mk": ("sbuf", [128, 128], B), "inc": ("sbuf", [128, 128], B), "sl": ("sbuf", [128, 128], F),
    "ta": ("sbuf", [128, 64], F), "tb": ("sbuf", [128, 32], F), "S": ("sbuf", [128, 16], I), "KI": ("sbuf", [128, 32], I),
    "KF": ("sbuf", [128, 32], F), "VI": ("sbuf", [128, 32], I), "VF": ("sbuf", [128, 32], F), "A": ("sbuf", [128, 2048], B),
    "ih": ("sbuf", [128, 72], B), "Bo": ("sbuf", [128, 1152], B), "WS": ("sbuf", [128, 64], F), "W": ("sbuf", [128, 64], B),
    "XS": ("sbuf", [128, 64], I), "XL": ("sbuf", [128, 64], I), "oi": ("sbuf", [128, 128], I), "off": ("sbuf", [128, 64], U),
    "rid": ("sbuf", [128, 64], U), "mm": ("sbuf", [128, 1024], B), "xm": ("sbuf", [128, 1024], F),
    "VS": ("sbuf", [128, 32], F), "VL": ("sbuf", [128, 32], F),
    "kk": ("sbuf", [128, 64], I), "kj": ("sbuf", [128, 32], F), "AJ": ("sbuf", [128, 2048], B), "AT": ("sbuf", [128, 2048], B),
    "BN": ("sbuf", [128, 512], B), "vv": ("sbuf", [128, 64], B), "prod": ("sbuf", [128, 512], F), "acc": ("sbuf", [128, 512], F),
    "LS": ("sbuf", [128, 256], U), "TL": ("sbuf", [128, 256], U), "rf": ("sbuf", [128, 128], F), "fin": ("sbuf", [128, 128], U),
    "SB": ("sbuf", [128, 4096], B), "D2": ("sbuf", [128, 4096], B), "Y": ("sbuf", [128, 2048], B),
    "PA": ("psum", [128, 512], F), "PB": ("psum", [128, 512], F), "PC": ("psum", [128, 512], F),
    "PF": ("psum", [128, 1024], F), "PX": ("psum", [128, 512], F), "PT": ("psum", [128, 2048], B),
}
SEMAPHORES = ["ev", "ea", "ep", "eg", "li", "lm", "lt", "st", "ax", "av", "ad", "s1", "s2", "s3", "s4"] + ["al%d" % _i for _i in range(8)]


def rank_program(g, core, T, topo):
    me = T.rank_of(core)
    if me is None:
        return
    cores, N = T.cores, len(T.cores)
    eng = {"v": g.vector, "a": g.scalar, "p": g.tensor, "g": g, "s": g.sync}
    cnt = {"v": 0, "a": 0, "p": 0, "g": 0}
    seen = {}

    def need(q, *toks):
        for name, val in toks:
            if seen.get((q, name), 0) < val:
                eng[q].wait_ge(T.sem[name], val)
                seen[(q, name)] = val

    def done(q, ins):
        cnt[q] += 1
        ins.then_inc(T.sem["e" + q], 1)
        return ("e" + q, cnt[q])

    def now(q):
        return ("e" + q, cnt[q])

    def ts(out, in0, s1, s2, op0, op1=None):
        if op1 is None:
            return done("v", g.vector.tensor_scalar(out, in0, s1, s2, op0))
        return done("v", g.vector.tensor_scalar(out, in0, s1, s2, op0, op1))

    def tt(out, a, b, op):
        return done("v", g.vector.tensor_tensor(out, a, b, op))

    def cp(out, a):
        return done("v", g.vector.tensor_copy(out, a))

    def act(out, a, f, **kw):
        return done("a", g.scalar.activation(out, a, f, **kw))

    def mat(out, l, r, start=True, stop=True):
        return g.tensor.matmul(out, l, r, start, stop)

    def same_chip(a, b):
        return topo.host(a) == topo.host(b) and topo.chip(a) == topo.chip(b)

    def order(r):
        c = cores[r]
        both, sw, mate, chip = [], [], [], []
        for k in range(1, N):
            s = (r + k) % N
            d = cores[s]
            (chip if same_chip(c, d) else mate if topo.mates(c, d) else sw if topo.same_plane(c, d) else both).append(s)
        return both + [x for p in zip(sw, mate) for x in p] + chip + [r]
    ords = [order(r) for r in range(N)]
    mine = ords[me]

    def pos(o, r):
        return ords[o].index(r)

    def bits(m):
        return [1 << i for i in range(16) if m >> i & 1]

    far = [r for r in mine if r != me and not same_chip(core, cores[r])]
    near = [r for r in mine if r != me and same_chip(core, cores[r])]
    eoff = bits(topo.mask(core, cores[far[0]]))
    eon = [e for e in bits(topo.mask(core, cores[near[0]])) if e not in eoff][:4]
    groups = [(far[:4], 2), (far[4:], 4)]

    def engines_for(src, dst):
        o = [r for r in ords[src] if r != src and not same_chip(cores[src], cores[r])]
        return 2 if dst in o[:4] else 4

    def fused(jobs, sem, local):
        tr, tot = [], 0
        for r, es, s, d in jobs:
            rid, pnc = topo.addr(cores[r], core)
            tr.append(RemoteDMATransfer(dst_ids=[DstId(rid=rid, pnc=pnc)], dma_engine_mask=sum(es), remote_sem=T.sem[sem(r)], src=s, dst=d))
            tot += len(es)
        g.remote_dma_fused(tr, local_sem=T.sem[local])
        return tot

    def control(which, item, sem, local):
        ds, w = groups[which]
        jobs = [(r, eoff[i * w:(i + 1) * w]) + item(r) for i, r in enumerate(ds)]
        if which == 1:
            jobs += [(r, eon) + item(r) for r in near]
        return fused(jobs, sem, local)
    arrive = sum(engines_for(s, me) for s in range(N) if s != me)

    g.sync.dma_start(T.E[:], T.idx[:]).then_inc(T.sem.li, 16)
    for v in range(2):
        for u in range(4):
            p0 = 32 * u + 16 * v
            g.sync.dma_start(T.mpw[p0:p0 + 16, 4:8196], T.mp[:, 8192 * v:8192 * v + 8192]).then_inc(T.sem.lm, 16)

    names = ["cO", "c4O", "cT", "rst", "i128", "neg1", "ntri", "ident", "ckA", "L2", "ones"]
    C = {n: T.cb[:, 128 * i:128 * i + 128] for i, n in enumerate(names)}
    ones = C["ones"]
    i64 = T.cb[:, 128 * names.index("i128"):128 * names.index("i128") + 64]
    i4 = T.cb[:, 128 * names.index("i128"):128 * names.index("i128") + 4]
    pint, pint1, rep1i, repi = T.ci[:, 0:8], T.ci[:, 0:1], T.ci[:, 16:24], T.ci[:, 32:64]

    def pbit(k):
        return T.ci[:, 8 + k:9 + k]

    def pcol(k):
        return T.cf[:, k:k + 1]
    w512, w256, cst, selu = T.cf[:, 8:9], T.cf[:, 9:10], T.cf[:, 10:11], T.cf[:, 12:16]
    i32r, rst32 = T.c5[:, 0:512], T.c5[:, 512:1024]
    mskb, self32 = T.cg[:, 0:128], T.cg[:, 128:256]
    rep1, repn = T.cu[:, 0:8], T.cu[:, 8:40]

    def iota(buf, pattern, base, cm):
        return done("g", g.iota(buf, pattern, base, cm, allow_small_or_imprecise_dtypes=True))
    m_neg = done("v", g.vector.memset(C["neg1"], -1.0))
    m_ones = done("v", g.vector.memset(ones, 1.0))
    done("v", g.vector.memset(T.mpw[:, 3:4], 0))
    m_zero = done("v", g.vector.memset(T.mpw[:, 8196:8197], 0))
    k_pint = iota(pint, [[0, 8]], 0, 1)
    k_cO = iota(C["cO"], [[1, 8], [0, 16]], 0, 0)
    k_cT = iota(C["cT"], [[0, 8], [1, 16]], 0, 0)
    need("g", m_neg)
    k_ntri = done("g", g.affine_select(C["ntri"], C["neg1"], [[-1, 128]], OP.is_ge, 0.0, 0, 1))
    k_i128 = iota(C["i128"], [[1, 128]], 0, 0)
    k_ih = iota(T.ih[:], [[2, 72]], -1, 0)
    k_ckA = iota(C["ckA"], [[16, 4], [0, 2], [1, 16]], 0, 0)
    need("g", m_ones)
    k_id = done("g", g.affine_select(C["ident"], ones, [[-1, 128]], OP.is_equal, 0.0, 0, 1))
    k_repi = iota(repi, [[1, 16], [0, 2]], 0, 0)

    need("v", k_pint)
    t_r1 = ts(rep1i, pint, 15, None, OP.bitwise_and)
    ts(pbit(0), pint1, 63, None, OP.bitwise_and)
    ts(pbit(1), pint1, 4, 1, OP.logical_shift_right, OP.bitwise_and)
    ts(pbit(2), pint1, 5, None, OP.logical_shift_right)
    ts(pbit(3), pint1, 7, None, OP.bitwise_and)
    ts(pbit(4), pint1, 3, None, OP.logical_shift_right)
    ts(pbit(5), pint1, 6, None, OP.logical_shift_right)
    t_pb = ts(T.ci[:, 14:16], T.ci[:, 0:2], 15, None, OP.bitwise_and)
    need("v", t_pb)
    t_rep1 = cp(rep1, rep1i)
    t_pc = cp(T.cf[:, 0:8], T.ci[:, 8:16])
    need("v", k_cO)
    k_c4O = ts(C["c4O"], C["cO"], 4.0, None, OP.mult)
    need("v", t_pc)
    ts(w256, pcol(5), -127.5, 128.0, OP.mult, OP.add)
    t_w = ts(w512, pcol(5), -255.5, 256.0, OP.mult, OP.add)
    t_cst = ts(cst, pcol(1), -131072.0, 131344.0, OP.mult, OP.add)
    need("v", k_cT)
    t_rst = ts(C["rst"], C["cT"], 1.0, None, OP.min)

    def compact(P, tok, oshift, values, onesb):
        KF, VF, A, Bo = T.KF, T.VF, T.A, T.Bo
        need("v", tok)
        x = ts(T.O[:], P[:], oshift, None, OP.logical_shift_right)
        need("v", x, t_rep1, k_cO)
        k = tt(T.mk[:], T.O[:, 0:16].indirect(rep1), C["cO"], OP.is_equal)
        need("v", k, t_rst)
        n = done("v", g.vector.tensor_tensor_scan(T.inc[:], C["rst"], T.mk[:], 0.0, OP.mult, OP.add))
        need("p", m_ones, k_c4O, k_ntri, k)
        mat(T.PA[:, 0:128], onesb, C["c4O"], True, False)
        mat(T.PA[:, 0:128], C["ntri"], T.mk[:], False, False)
        need("p", n)
        r = done("p", mat(T.PA[:, 0:128], onesb, T.inc[:], False, True))
        values(T.VI, VF)
        need("v", r)
        x = tt(T.sl[:], T.mk[:], T.PA[:, 0:128], OP.mult)
        need("v", x)
        x = tt(T.ta[:], T.sl[:, 0:64], T.sl[:, 64:128], OP.add)
        need("v", x)
        x = tt(T.tb[:], T.ta[:, 0:32], T.ta[:, 32:64], OP.add)
        need("v", x)
        x = tt(T.S[:], T.tb[:, 0:16], T.tb[:, 16:32], OP.add)
        need("v", x)
        ts(T.KI[:, 16:32], T.S[:], 6, None, OP.logical_shift_right)
        x = ts(T.KI[:, 0:16], T.S[:], 63, None, OP.bitwise_and)
        need("v", x)
        kf = cp(KF[:], T.KI[:])
        need("a", kf, k_ih)
        btok = [act(Bo[:, 72 * t:72 * t + 65], T.ih[:, 0:65], AF.Sign, bias=KF[:, 16 + t:17 + t], scale=-0.5) for t in range(16)]
        need("v", kf, k_i128)
        atok = []
        for t in range(16):
            ts(A[:, 128 * t:128 * t + 64], i64, KF[:, t:t + 1], VF[:, 16 + t:17 + t], OP.is_equal, OP.mult)
            atok.append(ts(A[:, 128 * t + 64:128 * t + 128], i64, KF[:, t:t + 1], VF[:, t:t + 1], OP.is_equal, OP.mult))
        for t in range(16):
            need("p", atok[t], btok[t])
            m = mat(T.PB[:, 0:65], A[:, 128 * t:128 * t + 128], Bo[:, 72 * t:72 * t + 65], t == 0, t == 15)
        m = done("p", m)
        need("v", m)
        x = cp(T.WS[:], T.PB[:, 0:64])
        need("v", x)
        return tt(T.W[:], T.WS[:], T.PB[:, 1:65], OP.subtract)

    def values1(VI, VF):
        ts(VI[:, 0:16], T.E[:], 511, None, OP.bitwise_and)
        x = ts(VI[:, 16:32], T.E[:], 9, 511, OP.logical_shift_right, OP.bitwise_and)
        need("v", x)
        ts(VF[:], VI[:], -256.0, None, OP.add)
        need("v", t_w, k_ckA)
        x = ts(C["L2"], C["ckA"], pcol(0), w512, OP.is_equal, OP.mult)
        need("v", x)

    w1 = compact(T.E, ("li", 16), 18, values1, ones)
    need("p", w1)
    x = done("p", mat(T.PC[:, 0:64], C["L2"], T.W[:]))
    need("v", x, t_cst)
    x1 = ts(T.XS[:], T.PC[:, 0:64], cst, None, OP.add)
    need("g", x1)
    tot = 0
    for w in range(2):
        tot += control(w, lambda r: (T.XS[:, 8 * r:8 * r + 8], T.XL[:, 8 * pos(r, me):8 * pos(r, me) + 8]), lambda r: "ax", "s1")
    k_i32 = iota(i32r, [[0, 16], [1, 32]], 0, 0)
    need("v", x1)
    own = cp(T.XL[:, 56:64], T.XS[:, 8 * me:8 * me + 8])
    need("s", ("s1", tot))
    g.sync.dma_start(T.tabw[:, 0:4096], T.tab[:, 0:4096]).then_inc(T.sem.lt, 16)

    ts(T.kk[:, 0:16], T.S[:], 2, 112, OP.logical_shift_right, OP.bitwise_and)
    ts(T.kk[:, 16:32], T.S[:], 7, 28, OP.logical_shift_right, OP.bitwise_and)
    ts(T.kk[:, 32:48], T.S[:], 15, None, OP.bitwise_and)
    x = ts(T.kk[:, 48:64], T.S[:], 4, 3, OP.logical_shift_right, OP.bitwise_and)
    need("v", x)
    x = tt(T.kj[:], T.kk[:, 0:32], T.kk[:, 32:64], OP.add)
    ts(selu, i4, pcol(2), None, OP.is_equal)
    k_wc = ts(T.wc[:], C["cT"][:, 0:16], pcol(6), None, OP.is_equal)
    need("v", k_repi)
    rn = cp(repn, repi)
    need("v", x)
    jt = []
    for t in range(16):
        jt.append(ts(T.AJ[:, 128 * t:128 * t + 128], C["i128"], T.kj[:, t:t + 1], None, OP.is_equal))
    at = []
    need("p", k_id)
    for rd in range(2):
        for t in range(8 * rd, 8 * rd + 8):
            need("p", jt[t])
            m = g.tensor.transpose(T.PT[:, 128 * t:128 * t + 128], T.AJ[:, 128 * t:128 * t + 128], C["ident"])
        m = done("p", m)
        a, b = 1024 * rd, 1024 * rd + 1024
        if rd:
            need("v", m)
            at.append(cp(T.AT[:, a:b], T.PT[:, a:b]))
        else:
            need("a", m)
            at.append(act(T.AT[:, a:b], T.PT[:, a:b], AF.Copy))

    need("v", ("ax", arrive), own)
    ri = ts(T.oi[:, 0:64], T.XL[:], 15, None, OP.bitwise_and)
    ci = ts(T.oi[:, 64:128], T.XL[:], 4, None, OP.arith_shift_right)
    need("v", ri)
    rd = cp(T.rid[:], T.oi[:, 0:64])
    need("v", ci)
    of = ts(T.off[:], T.oi[:, 64:128], 0.0, 8193.0, OP.max, OP.min)
    need("a", rd, k_wc)
    parts = [(0, 1), (1, 2), (2, 4), (4, 6), (6, 8)]
    mt = [act(T.mm[:, 128 * a:128 * b], T.wc[:, 0:16].indirect(T.rid[:, 8 * a:8 * b]), AF.Copy) for a, b in parts]
    need("v", of, ("lm", 128), m_zero)
    ft = []
    for (a, b), m in zip(parts, mt):
        need("v", m)
        x = tt(T.xm[:, 128 * a:128 * b], T.mpw[:, 3:8197].indirect(T.off[:, 8 * a:8 * b]), T.mm[:, 128 * a:128 * b], OP.mult)
        need("p", x)
        for r in range(a, b):
            PV = T.PA if r >= 4 else T.PB
            m = mat(PV[:, 4 * (r % 4):4 * (r % 4) + 4], T.xm[:, 128 * r:128 * r + 128], selu)
        if b in (4, 8):
            ft.append(done("p", m))
    s2tot = 0
    for h in range(2):
        PV = T.PA if h else T.PB
        need("a", ft[h])
        vs = act(T.VS[:, 16 * h:16 * h + 16], PV[:, 0:16], AF.Copy)
        need("g", vs)
        s2tot += control(h, lambda r: (T.VS[:, 4 * mine.index(r):4 * mine.index(r) + 4], T.VL[:, 4 * me:4 * me + 4]), lambda r: "av", "s2")
    need("s", ("s2", s2tot))
    g.sync.dma_start(T.tabw[:, 4096:8192], T.tab[:, 4096:8192]).then_inc(T.sem.lt, 16)
    need("v", vs)
    own = cp(T.VL[:, 4 * me:4 * me + 4], T.VS[:, 28:32])

    need("v", rn, k_i32)
    bn = tt(T.BN[:], T.kj[:, 16:32].indirect(repn), i32r, OP.is_equal)
    r32 = ts(rst32, i32r, 1.0, None, OP.min)
    for u in range(4):
        x = ts(T.cf[:, 32 + u:33 + u], pcol(0), float(-16 * u), None, OP.add)
    need("v", x)
    for u in range(4):
        ts(T.LU[:, 128 * u:128 * u + 128], C["cT"], T.cf[:, 32 + u:33 + u], w256, OP.is_equal, OP.mult)
    ts(mskb, C["cO"], pcol(3), None, OP.is_equal)
    k_late = ts(self32, C["cT"], pcol(4), None, OP.is_equal)

    vh, vl = T.vv[:, 0:32], T.vv[:, 32:64]
    need("v", ("av", arrive), own)
    x = cp(vh, T.VL[:])
    need("v", x)
    x = tt(vl, T.VL[:], vh, OP.subtract)
    need("p", x, *at)
    PQ = [T.PF[:, 0:128], T.PX[:, 0:128], T.PF[:, 512:640], T.PC[:, 0:128]]
    zt = []
    for t in range(16):
        z = PQ[t // 4][:, 32 * (t % 4):32 * (t % 4) + 32]
        mat(z, T.AT[:, 128 * t:128 * t + 128], vh, True, False)
        m = mat(z, T.AT[:, 128 * t:128 * t + 128], vl, False, True)
        if t % 4 == 3:
            zt.append(done("p", m))
    need("v", bn, r32)
    for k in range(4):
        c0, c1 = 128 * k, 128 * k + 128
        need("v", zt[k])
        x = tt(T.prod[:, c0:c1], T.BN[:, c0:c1], PQ[k], OP.mult)
        need("v", x)
        x = done("v", g.vector.tensor_tensor_scan(T.acc[:, c0:c1], rst32[:, c0:c1], T.prod[:, c0:c1], 0.0, OP.mult, OP.add))
    need("v", x)
    val = cp(T.VAL[:], T.acc[:, 31:512:32])

    def values2(VI, VF):
        ts(VI[:, 0:16], T.VAL[:], 255, None, OP.bitwise_and)
        x = ts(VI[:, 16:32], T.VAL[:], 8, 31, OP.logical_shift_right, OP.bitwise_and)
        need("v", x)
        x = cp(VF[:], VI[:])
        need("v", x)

    need("p", k_late)
    w2 = compact(T.VAL, val, 13, values2, ones)
    need("p", w2)
    for u in range(4):
        m = mat(T.PC[:, u:256:4], T.LU[:, 128 * u:128 * u + 128], T.W[:])
    m = done("p", m)
    need("v", m)
    ls = cp(T.LS[:], T.PC[:, 0:256])
    need("g", ls)
    s3tot = 0
    for w in range(2):
        s3tot += control(w, lambda r: (T.LS[:, 32 * r:32 * r + 32], T.TL[:, 32 * pos(r, me):32 * pos(r, me) + 32]), lambda r: "al%d" % pos(r, me), "s3")
    x = tt(T.rf[:], T.S[:, 0:16].indirect(rep1), mskb, OP.mult)
    need("p", x)
    m = done("p", mat(T.PA[:, 0:128], self32, T.rf[:]))
    need("v", m)
    fin = cp(T.fin[:], T.PA[:, 0:128])

    sent = 0
    for i in range(2):
        r, toks = mine[i], []
        for k in range(2):
            q = "va"[k]
            need(q, ("al%d" % i, engines_for(r, me)), ("lt", 32))
            c0 = 512 * i + 256 * k
            win, out = T.tabw[:, 0:8192].indirect(T.TL[:, c0 // 16:c0 // 16 + 16]), T.SB[:, c0:c0 + 256]
            toks.append(cp(out, win) if q == "v" else act(out, win, AF.Copy))
        need("g", *toks)
        sent += fused([(r, eoff[i::2], T.SB[:, 512 * i:512 * i + 512], T.D2[:, 512 * me:512 * me + 512])], lambda r: "ad", "s4")
    for i in range(2, 8, 2):
        jobs, toks = [], []
        for k in range(2):
            r, q = mine[i + k], "va"[k]
            if r == me:
                need(q, ls)
                lst, out = T.LS[:, 32 * me:32 * me + 32], T.D2[:, 512 * me:512 * me + 512]
            else:
                need(q, ("al%d" % (i + k), engines_for(r, me)))
                lst, out = T.TL[:, 32 * (i + k):32 * (i + k) + 32], T.SB[:, 512 * (i + k):512 * (i + k) + 512]
                jobs.append((r, eon if r in near else eoff[k::2], out, T.D2[:, 512 * me:512 * me + 512]))
            win = T.tabw[:, 0:8192].indirect(lst)
            x = cp(out, win) if q == "v" else act(out, win, AF.Copy)
            if r == me:
                dself = x
            else:
                toks.append(x)
        need("g", *toks)
        sent += fused(jobs, lambda r: "ad", "s4")
    dat = sum(len(eoff) // 2 if not same_chip(cores[s], core) else len(eon) for s in range(N) if s != me)

    for i, (c0, c1) in enumerate([(0, 640), (640, 1280), (1280, 1664), (1664, 2048)]):
        q = "va"[i % 2]
        need(q, dself, fin, ("ad", dat))
        win = T.D2[:, 0:4096].indirect(T.fin[:, c0 // 16:c1 // 16])
        out = T.Y[:, c0:c1]
        x = cp(out, win) if q == "v" else act(out, win, AF.Copy)
        need("s", x)
        g.sync.dma_start(T.y[:, c0:c1], out).then_inc(T.sem.st, 16)
    need("s", ("st", 64))
    need("g", ("s2", s2tot), ("s3", s3tot), ("s4", sent), now("v"), now("a"), now("p"), now("g"))
